import numpy as np
import ml_dtypes


def mxq(x, axis, fmt="e4m3"):
    dtype, down = {"e4m3": (ml_dtypes.float8_e4m3fn, 7), "e5m2": (ml_dtypes.float8_e5m2, 14)}[fmt]
    v = np.moveaxis(np.asarray(x, np.float32).astype(ml_dtypes.bfloat16).astype(np.float64), axis, -1)
    blocks = v.reshape(v.shape[:-1] + (-1, 32))
    amax = np.abs(blocks).max(-1, keepdims=True)
    byte = np.maximum(np.where(amax > 0, np.frexp(amax)[1] - 1 + 127, 0) - down, 1)
    scale = np.exp2(byte - 127.0)
    codes = (blocks / scale).astype(np.float32).astype(dtype).astype(np.float64)
    return np.moveaxis((codes * scale).reshape(v.shape), -1, axis)


WIDE = False


def mx_kscale(k):
    if not WIDE:
        return np.ones(k)
    levels = np.array([10, -10, 5, -5, 0])
    if k % 512:
        return np.exp2(np.random.permutation(np.resize(levels, k // 32))).repeat(32)
    a = np.empty((k // 512, 16))
    for p in range(k // 512):
        a[p, :8] = np.random.permutation(np.resize(levels, 8))
        for g in range(8):
            far = levels[np.abs(levels - a[p, g]) >= 10]
            a[p, g + 8] = far[np.random.randint(len(far))]
    return np.exp2(a.ravel()).repeat(32)


BF16 = ml_dtypes.bfloat16


def bf(x):
    return np.asarray(x, np.float32).astype(BF16)


def f64(x):
    return np.asarray(x).astype(np.float64)


E2M1 = np.array([0.0, 0.5, 1.0, 1.5, 2.0, 3.0, 4.0, 6.0, -0.0, -0.5, -1.0, -1.5, -2.0, -3.0, -4.0, -6.0])


def pack_weight(w, fmt):
    k, n = w.shape
    w = f64(bf(w)).reshape(k // 32, 32, n)
    amax = np.abs(w).max(1)
    if fmt == "e4m3":
        byte = np.frexp(amax)[1] - 1 + 127 - 7
    else:
        mant, ex = np.frexp(amax / 6.0)
        byte = np.where(mant > 0.5, ex, ex - 1) + 127
    byte = np.clip(np.where(amax > 0, byte, 1), 1, 254)
    scaled = (w * np.exp2(127.0 - byte)[:, None, :]).reshape(k, n).astype(np.float32)
    by_word = np.ascontiguousarray(scaled.reshape(k // 512, 128, 4, n).transpose(0, 1, 3, 2))
    if fmt == "e4m3":
        words = by_word.astype(ml_dtypes.float8_e4m3fn).view(np.uint8)
    else:
        c = by_word.astype(ml_dtypes.float4_e2m1fn).view(np.uint8) & 0xF
        words = c[..., 0::2] | (c[..., 1::2] << 4)
    return np.ascontiguousarray(words), np.ascontiguousarray(byte.astype(np.uint8).reshape(k // 512, 16, n))


def unpack_weight(words, scales, fmt):
    g, p, n, _ = words.shape
    if fmt == "e4m3":
        vals = np.ascontiguousarray(words).view(ml_dtypes.float8_e4m3fn).astype(np.float64)
    else:
        nib = np.empty((g, p, n, 4), np.uint8)
        nib[..., 0::2] = words & 0xF
        nib[..., 1::2] = words >> 4
        vals = E2M1[nib]
    vals = vals * np.repeat(np.exp2(scales.astype(np.float64) - 127.0), 8, axis=1)[..., None]
    return vals.transpose(0, 1, 3, 2).reshape(g * 512, n)
def pack4(w):
    words, scales = pack_weight(w, "e2m1")
    return words.reshape(words.shape[0], 128, -1), scales


def unpack4(words, scales):
    return unpack_weight(words.reshape(words.shape[0], 128, -1, 2), scales, "e2m1")


M, K, N = 2048, 1024, 1024


def draw0():
    s, t = mx_kscale(K), mx_kscale(M)
    hidden = np.random.standard_normal((M, K))
    h_words, h_scales = pack4(hidden / np.sqrt(M) / t[:, None])
    return {"x": bf(hidden * s),
            "w": bf(np.random.standard_normal((K, N)) / np.sqrt(K) / s[:, None]),
            "mean_logit": bf(1 + 0.3 * np.random.standard_normal(M)),
            "rel_prob": bf(np.exp(0.7 * np.random.standard_normal((M, N)))),
            "coef": bf(np.random.uniform(0.5, 1.5, M) * t),
            "h_words": h_words,
            "h_scales": h_scales}


def core(x, w, mean_logit, rel_prob, coef, h_words, h_scales):
    logits = mxq(f64(x), 1, "e4m3") @ mxq(f64(w), 0, "e4m3")
    deviation = logits - f64(mean_logit)[:, None]
    delta = deviation * f64(rel_prob) * f64(coef)[:, None]
    h = unpack4(h_words, h_scales)
    grad = h.T @ mxq(delta, 0, "e4m3")
    return grad


def e4m3fn_bytes(y):
    return np.clip(np.asarray(y, np.float64), -448.0, 448.0).astype(np.float32).astype(ml_dtypes.float8_e4m3fn).view(np.uint8)


def e4m3fn_values(b):
    return np.asarray(b, np.uint8).view(ml_dtypes.float8_e4m3fn).astype(np.float64)


def setup_inputs():
    d = draw0()
    x0 = np.asarray(d['x']).astype(np.float64)
    s = (np.max(np.abs(x0), axis=(0,), keepdims=True) / 448.0).astype(np.float32)
    out = {}
    for k, v in d.items():
        if k == 'x':
            out['x_bytes'] = e4m3fn_bytes(x0 / s.astype(np.float64))
            out['x_scale'] = s
        else:
            out[k] = v
    return out


def reference(x_bytes, x_scale, w, mean_logit, rel_prob, coef, h_words, h_scales):
    return core(e4m3fn_values(x_bytes) * x_scale.astype(np.float64), w, mean_logit, rel_prob, coef, h_words, h_scales)

@@ -1,0 +1,316 @@
+from contextlib import ExitStack
+
+import concourse.mybir as mybir
+from concourse.masks import make_identity
+
+TOKENS, HIDDEN, ACTIONS = 2048, 1024, 1024
+FLOPS = 2 * 2 * TOKENS * HIDDEN * ACTIONS
+
+F32 = mybir.dt.float32
+BF16 = mybir.dt.bfloat16
+I32 = mybir.dt.int32
+U32 = mybir.dt.uint32
+U8 = mybir.dt.uint8
+FP8 = mybir.dt.float8_e4m3fn
+FP8X4 = mybir.dt.float8_e4m3fn_x4
+FP4X4 = mybir.dt.float4_e2m1fn_x4
+MULT = mybir.AluOpType.mult
+IDENTITY = mybir.ActivationFunctionType.Identity
+
+P = 128
+GROUPS = TOKENS // 512
+TILES = TOKENS // P
+PASSES = HIDDEN // 512
+HALF = 512
+KTILES = HIDDEN // P
+
+
+def tile_entropy_bonus_gradient_s13_kernel(
+    tc, x_bytes, x_scale, w, mean_logit, rel_prob, coef, h_words, h_scales, out
+):
+    nc = tc.nc
+    with ExitStack() as ctx:
+        keep = ctx.enter_context(tc.tile_pool(name="keep", bufs=1))
+        work = ctx.enter_context(tc.tile_pool(name="work", bufs=3))
+        psum = ctx.enter_context(tc.psum_pool(name="psum", bufs=8))
+        ctx.enter_context(tc.manual_schedule())
+
+        ident = keep.tile([P, P], F32, name="ident")
+        scale_row = keep.tile([P, HIDDEN], F32, name="scale_row", align_bytes=64)
+        xb = [keep.tile([P, 4, HIDDEN], U8, name="xb%d" % g, align_bytes=64) for g in range(GROUPS)]
+        w_raw = {}
+        for h in range(2):
+            for c in range(PASSES):
+                w_raw[h, c] = keep.tile([P, 4, HALF], BF16, name="wr%d%d" % (h, c), align_bytes=64)
+        rel = [keep.tile([P, 4, ACTIONS], BF16, name="rel%d" % g, align_bytes=64) for g in range(GROUPS)]
+        hw = keep.tile([P, GROUPS, 2 * HIDDEN], U8, name="hw", align_bytes=64)
+        hs = keep.tile([P, GROUPS, HIDDEN], U8, name="hs", align_bytes=64)
+        mean_b = keep.tile([P, GROUPS, 4], BF16, name="mean_b")
+        coef_b = keep.tile([P, GROUPS, 4], BF16, name="coef_b")
+        coef_f = keep.tile([P, GROUPS, 4], F32, name="coef_f")
+        mc = keep.tile([P, GROUPS, 4], F32, name="mc")
+        nmc = keep.tile([P, GROUPS, 4], F32, name="nmc")
+        warm = keep.tile([P, 1], F32, name="warm")
+
+        xc = keep.tile([P, TILES, PASSES, P], U32, name="xc", align_bytes=64)
+        xs = keep.tile([P, TILES, PASSES, P], U8, name="xs", align_bytes=64)
+        wc = keep.tile([P, PASSES, ACTIONS], U32, name="wc", align_bytes=64)
+        ws = keep.tile([P, PASSES, ACTIONS], U8, name="ws", align_bytes=64)
+        dc = keep.tile([P, GROUPS, ACTIONS], U32, name="dc", align_bytes=64)
+        ds = keep.tile([P, GROUPS, ACTIONS], U8, name="ds", align_bytes=64)
+
+        def load_x(g, t0, t1):
+            nc.sync.dma_start(
+                out=xb[g][:, t0:t1, :],
+                in_=x_bytes[512 * g : 512 * (g + 1), :].rearrange("(p t) k -> p t k", t=4)[:, t0:t1, :],
+            )
+
+        def load_w(h, c):
+            nc.sync.dma_start(
+                out=w_raw[h, c][:],
+                in_=w[512 * c : 512 * (c + 1), HALF * h : HALF * (h + 1)].rearrange("(p j) n -> p j n", j=4),
+            )
+
+        def load_rel(g, t0, t1):
+            nc.sync.dma_start(
+                out=rel[g][:, t0:t1, :],
+                in_=rel_prob[512 * g : 512 * (g + 1), :].rearrange("(p t) n -> p t n", t=4)[:, t0:t1, :],
+            )
+
+        nc.scalar.dma_start(out=mean_b[:], in_=mean_logit.rearrange("(g p t) -> p g t", p=P, t=4))
+        nc.scalar.dma_start(out=coef_b[:], in_=coef.rearrange("(g p t) -> p g t", p=P, t=4))
+        make_identity(nc, ident[:])
+        nc.gpsimd.memset(warm[:], 0.0)
+        nc.scalar.activation(out=warm[:], in_=warm[:], func=IDENTITY)
+        nc.gpsimd.memset(hs[:].rearrange("p g n -> p (g n)").bitcast(U32), 0)
+        nc.gpsimd.tensor_copy(out=coef_f[:], in_=coef_b[:])
+        nc.gpsimd.tensor_tensor(out=mc[:], in0=mean_b[:], in1=coef_b[:], op=MULT)
+        nc.gpsimd.tensor_scalar(out=nmc[:], in0=mc[:], scalar1=-1.0, scalar2=None, op0=MULT)
+
+        nc.sync.dma_start(out=scale_row[:], in_=x_scale.rearrange("o k -> (o k)").partition_broadcast(P))
+        load_x(0, 0, 2)
+        load_w(0, 0)
+        load_w(0, 1)
+        load_x(0, 2, 4)
+        load_x(1, 0, 4)
+        load_x(2, 0, 4)
+        load_x(3, 0, 4)
+        load_w(1, 0)
+        load_w(1, 1)
+        for q in range(4):
+            nc.sync.dma_start(
+                out=hs[32 * q : 32 * q + 4].rearrange("p g n -> p (g n)").bitcast(I32).rearrange("p (g n) -> p g n", g=GROUPS),
+                in_=h_scales[:, 4 * q : 4 * q + 4, :].rearrange("g q n -> q g n").bitcast(I32),
+            )
+        load_rel(0, 0, 2)
+        load_rel(0, 2, 4)
+        load_rel(1, 0, 4)
+        nc.sync.dma_start(out=hw[:], in_=h_words.rearrange("g p c -> p g c"))
+        load_rel(2, 0, 4)
+        load_rel(3, 0, 4)
+
+        xw = {}
+        xt = {}
+        xg = {}
+        lg = {}
+        dg = {}
+
+        def widen(i):
+            xw[i] = work.tile([P, HIDDEN], BF16, name="xw", tag="xw", bufs=4, align_bytes=64)
+            nc.vector.tensor_tensor(
+                out=xw[i][:], in0=xb[i // 4][:, i % 4, :].bitcast(FP8), in1=scale_row[:], op=MULT
+            )
+
+        def turn(i):
+            xt[i] = psum.tile([P, 4, P], F32, name="bank", tag="bank", bufs=8)
+            words = xw[i][:].bitcast(F32)
+            for c in range(PASSES):
+                for u in range(2):
+                    nc.tensor.transpose(
+                        xt[i][:, 2 * c + u, :], words[:, 256 * c + u : 256 * (c + 1) : 2], ident[:]
+                    )
+
+        def untangle(i):
+            if i % 2 == 0:
+                xg[i // 2] = work.tile([P, 2, PASSES * P * 4], BF16, name="xg", tag="xg", bufs=3, align_bytes=64)
+            nc.scalar.copy(
+                out=xg[i // 2][:, i % 2, :].bitcast(F32).rearrange("p (c r u) -> p c r u", c=PASSES, u=2),
+                in_=xt[i][:].rearrange("p (c u) r -> p c r u", c=PASSES),
+            )
+
+        def quant_x(j):
+            nc.vector.quantize_mx(
+                out=xc[:, 2 * j : 2 * j + 2].rearrange("p a c r -> p (a c r)").bitcast(FP8X4),
+                scales=xs[:, 2 * j : 2 * j + 2].rearrange("p a c r -> p (a c r)"),
+                in_=xg[j][:].rearrange("p a f -> p (a f)"),
+            )
+
+        wg = {}
+
+        def group_w(h, c, engine):
+            wg[h, c] = work.tile([P, HALF, 4], BF16, name="wg", tag="wg", bufs=2, align_bytes=64)
+            dst = wg[h, c][:].rearrange("p (c i) j -> p c j i", i=4)
+            src = w_raw[h, c][:].rearrange("p j (c i) -> p c j i", i=4)
+            if engine == "v":
+                nc.vector.tensor_copy(out=dst, in_=src)
+            else:
+                nc.scalar.copy(out=dst, in_=src)
+
+        def quant_w(h, c):
+            cols = slice(HALF * h, HALF * (h + 1))
+            nc.vector.quantize_mx(
+                out=wc[:, c, cols].bitcast(FP8X4),
+                scales=ws[:, c, cols],
+                in_=wg[h, c][:].rearrange("p n j -> p (n j)"),
+            )
+
+        acc = {}
+
+        def logits(i, h):
+            acc[i, h] = psum.tile([P, HALF], F32, name="bank", tag="bank", bufs=8)
+            cols = slice(HALF * h, HALF * (h + 1))
+            for c in range(PASSES):
+                nc.tensor.matmul_mx(
+                    out=acc[i, h][:],
+                    lhsT=xc[:, i, c, :].bitcast(FP8X4),
+                    lhsT_scale=xs[:, i, c, :],
+                    rhs=wc[:, c, cols].bitcast(FP8X4),
+                    rhs_scale=ws[:, c, cols],
+                    start=(c == 0),
+                    stop=(c == PASSES - 1),
+                )
+
+        def deviate(i, h):
+            g, t = i // 4, i % 4
+            if t == 0:
+                lg[g, h] = work.tile([P, 4, HALF], F32, name="lg", tag="lg", bufs=6, align_bytes=64)
+            nc.scalar.activation(
+                out=lg[g, h][:, t, :],
+                in_=acc[i, h][:],
+                func=IDENTITY,
+                bias=nmc[:, g, t : t + 1],
+                scale=coef_f[:, g, t : t + 1],
+            )
+
+        def weight(g, h):
+            dg[g, h] = work.tile([P, HALF, 4], BF16, name="dg", tag="dg", bufs=3, align_bytes=64)
+            nc.vector.tensor_tensor(
+                out=dg[g, h][:].rearrange("p (c i) t -> p c t i", i=4),
+                in0=lg[g, h][:].rearrange("p t (c i) -> p c t i", i=4),
+                in1=rel[g][:, :, HALF * h : HALF * (h + 1)].rearrange("p t (c i) -> p c t i", i=4),
+                op=MULT,
+            )
+
+        def quant_d(g, h):
+            cols = slice(HALF * h, HALF * (h + 1))
+            nc.vector.quantize_mx(
+                out=dc[:, g, cols].bitcast(FP8X4),
+                scales=ds[:, g, cols],
+                in_=dg[g, h][:].rearrange("p n t -> p (n t)"),
+            )
+
+        grad = {}
+
+        def gradient(k, h, g):
+            if g == 0:
+                grad[k, h] = psum.tile([P, HALF], F32, name="bank", tag="bank", bufs=8)
+            cols = slice(HALF * h, HALF * (h + 1))
+            nc.tensor.matmul_mx(
+                out=grad[k, h][:],
+                lhsT=hw[:, g, 2 * P * k : 2 * P * (k + 1)].bitcast(FP4X4),
+                lhsT_scale=hs[:, g, P * k : P * (k + 1)],
+                rhs=dc[:, g, cols].bitcast(FP8X4),
+                rhs_scale=ds[:, g, cols],
+                start=(g == 0),
+                stop=(g == GROUPS - 1),
+            )
+
+        def finish(k, h, engine):
+            res = work.tile([P, HALF], F32, name="res", tag="res", bufs=6, align_bytes=64)
+            if engine == "v":
+                nc.vector.tensor_copy(out=res[:], in_=grad[k, h][:])
+            else:
+                nc.scalar.copy(out=res[:], in_=grad[k, h][:])
+            nc.sync.dma_start(out=out[P * k : P * (k + 1), HALF * h : HALF * (h + 1)], in_=res[:])
+
+        def pair_logits(j, h):
+            logits(2 * j, h)
+            logits(2 * j + 1, h)
+            deviate(2 * j, h)
+            deviate(2 * j + 1, h)
+
+        def open_half(g):
+            for k in range(4):
+                gradient(k, 0, g)
+
+        def all_half(g):
+            for k in range(8):
+                gradient(k, 1, g)
+
+        group_w(0, 0, "s")
+        for j in range(8):
+            widen(2 * j)
+            widen(2 * j + 1)
+            if j == 0:
+                group_w(0, 1, "v")
+            if j == 1:
+                quant_w(0, 0)
+            turn(2 * j)
+            turn(2 * j + 1)
+            untangle(2 * j)
+            untangle(2 * j + 1)
+            if j == 1:
+                quant_x(0)
+                quant_w(0, 1)
+            elif j > 1:
+                quant_x(j - 1)
+            if j in (4, 6):
+                quant_d(j // 2 - 2, 0)
+            if j > 0:
+                pair_logits(j - 1, 0)
+            if j == 1:
+                group_w(1, 0, "s")
+            if j == 2:
+                group_w(1, 1, "v")
+                quant_w(1, 0)
+            if j == 3:
+                quant_w(1, 1)
+            if j in (3, 5, 7):
+                weight(j // 2 - 1, 0)
+            if j >= 4:
+                pair_logits(j - 4, 1)
+            if j == 5:
+                open_half(0)
+            if j == 7:
+                pair_logits(4, 1)
+                open_half(1)
+        quant_x(7)
+        pair_logits(7, 0)
+        weight(0, 1)
+        quant_d(2, 0)
+        pair_logits(5, 1)
+        open_half(2)
+        weight(3, 0)
+        quant_d(0, 1)
+        weight(1, 1)
+        quant_d(3, 0)
+        pair_logits(6, 1)
+        pair_logits(7, 1)
+        for k in range(4):
+            gradient(k, 0, 3)
+            finish(k, 0, "s")
+        weight(2, 1)
+        quant_d(1, 1)
+        for k in range(4, 8):
+            for g in range(GROUPS):
+                gradient(k, 0, g)
+            finish(k, 0, "s")
+        all_half(0)
+        weight(3, 1)
+        quant_d(2, 1)
+        all_half(1)
+        quant_d(3, 1)
+        all_half(2)
+        for k in range(8):
+            gradient(k, 1, 3)
+            finish(k, 1, "v" if k % 2 == 0 else "s")

@@ -22,7 +22,7 @@ GROUPS = TOKENS // 512
 TILES = TOKENS // P
 PASSES = HIDDEN // 512
 HALF = 512
-KTILES = HIDDEN // P
+CHUNKS = [slice(0, 512), slice(512, 1024)]
 
 
 def tile_entropy_bonus_gradient_s13_kernel(
@@ -192,31 +192,34 @@ def tile_entropy_bonus_gradient_s13_kernel(
                 scale=coef_f[:, g, t : t + 1],
             )
 
-        def weight(g, h):
-            dg[g, h] = work.tile([P, HALF, 4], BF16, name="dg", tag="dg", bufs=3, align_bytes=64)
+        def weight(g, q):
+            cols = CHUNKS[q]
+            width = cols.stop - cols.start
+            h = cols.start // HALF
+            dg[g, q] = work.tile([P, width, 4], BF16, name="dg", tag="dg", bufs=3, align_bytes=64)
             nc.vector.tensor_tensor(
-                out=dg[g, h][:].rearrange("p (c i) t -> p c t i", i=4),
-                in0=lg[g, h][:].rearrange("p t (c i) -> p c t i", i=4),
-                in1=rel[g][:, :, HALF * h : HALF * (h + 1)].rearrange("p t (c i) -> p c t i", i=4),
+                out=dg[g, q][:].rearrange("p (c i) t -> p c t i", i=4),
+                in0=lg[g, h][:, :, cols.start - HALF * h : cols.stop - HALF * h].rearrange("p t (c i) -> p c t i", i=4),
+                in1=rel[g][:, :, cols].rearrange("p t (c i) -> p c t i", i=4),
                 op=MULT,
             )
 
-        def quant_d(g, h):
-            cols = slice(HALF * h, HALF * (h + 1))
+        def quant_d(g, q):
+            cols = CHUNKS[q]
             nc.vector.quantize_mx(
                 out=dc[:, g, cols].bitcast(FP8X4),
                 scales=ds[:, g, cols],
-                in_=dg[g, h][:].rearrange("p n t -> p (n t)"),
+                in_=dg[g, q][:].rearrange("p n t -> p (n t)"),
             )
 
         grad = {}
 
-        def gradient(k, h, g):
+        def gradient(k, q, g):
+            cols = CHUNKS[q]
             if g == 0:
-                grad[k, h] = psum.tile([P, HALF], F32, name="bank", tag="bank", bufs=8)
-            cols = slice(HALF * h, HALF * (h + 1))
+                grad[k, q] = psum.tile([P, cols.stop - cols.start], F32, name="bank", tag="bank", bufs=8)
             nc.tensor.matmul_mx(
-                out=grad[k, h][:],
+                out=grad[k, q][:],
                 lhsT=hw[:, g, 2 * P * k : 2 * P * (k + 1)].bitcast(FP4X4),
                 lhsT_scale=hs[:, g, P * k : P * (k + 1)],
                 rhs=dc[:, g, cols].bitcast(FP8X4),
@@ -225,13 +228,14 @@ def tile_entropy_bonus_gradient_s13_kernel(
                 stop=(g == GROUPS - 1),
             )
 
-        def finish(k, h, engine):
-            res = work.tile([P, HALF], F32, name="res", tag="res", bufs=6, align_bytes=64)
+        def finish(k, q, engine):
+            cols = CHUNKS[q]
+            res = work.tile([P, cols.stop - cols.start], F32, name="res", tag="res", bufs=8, align_bytes=64)
             if engine == "v":
-                nc.vector.tensor_copy(out=res[:], in_=grad[k, h][:])
+                nc.vector.tensor_copy(out=res[:], in_=grad[k, q][:])
             else:
-                nc.scalar.copy(out=res[:], in_=grad[k, h][:])
-            nc.sync.dma_start(out=out[P * k : P * (k + 1), HALF * h : HALF * (h + 1)], in_=res[:])
+                nc.scalar.copy(out=res[:], in_=grad[k, q][:])
+            nc.sync.dma_start(out=out[P * k : P * (k + 1), cols], in_=res[:])
 
         def pair_logits(j, h):
             logits(2 * j, h)
@@ -239,78 +243,227 @@ def tile_entropy_bonus_gradient_s13_kernel(
             deviate(2 * j, h)
             deviate(2 * j + 1, h)
 
-        def open_half(g):
-            for k in range(4):
-                gradient(k, 0, g)
-
-        def all_half(g):
-            for k in range(8):
-                gradient(k, 1, g)
-
+        widen(0)
+        widen(1)
+        widen(2)
+        widen(3)
+        turn(0)
+        turn(1)
+        turn(2)
+        turn(3)
         group_w(0, 0, "s")
-        for j in range(8):
-            widen(2 * j)
-            widen(2 * j + 1)
-            if j == 0:
-                group_w(0, 1, "v")
-            if j == 1:
-                quant_w(0, 0)
-            turn(2 * j)
-            turn(2 * j + 1)
-            untangle(2 * j)
-            untangle(2 * j + 1)
-            if j == 1:
-                quant_x(0)
-                quant_w(0, 1)
-            elif j > 1:
-                quant_x(j - 1)
-            if j in (4, 6):
-                quant_d(j // 2 - 2, 0)
-            if j > 0:
-                pair_logits(j - 1, 0)
-            if j == 1:
-                group_w(1, 0, "s")
-            if j == 2:
-                group_w(1, 1, "v")
-                quant_w(1, 0)
-            if j == 3:
-                quant_w(1, 1)
-            if j in (3, 5, 7):
-                weight(j // 2 - 1, 0)
-            if j >= 4:
-                pair_logits(j - 4, 1)
-            if j == 5:
-                open_half(0)
-            if j == 7:
-                pair_logits(4, 1)
-                open_half(1)
+        untangle(0)
+        untangle(1)
+        group_w(0, 1, "s")
+        untangle(2)
+        untangle(3)
+        group_w(1, 0, "s")
+        quant_w(0, 0)
+        widen(4)
+        widen(5)
+        quant_w(0, 1)
+        quant_x(0)
+        widen(6)
+        widen(7)
+        quant_x(1)
+        turn(4)
+        turn(5)
+        turn(6)
+        turn(7)
+        logits(0, 0)
+        logits(1, 0)
+        logits(2, 0)
+        logits(3, 0)
+        untangle(4)
+        untangle(5)
+        untangle(6)
+        untangle(7)
+        group_w(1, 1, "s")
+        deviate(0, 0)
+        deviate(1, 0)
+        deviate(2, 0)
+        deviate(3, 0)
+        quant_x(2)
+        widen(8)
+        widen(9)
+        quant_w(1, 0)
+        quant_x(3)
+        widen(10)
+        widen(11)
+        quant_w(1, 1)
+        turn(8)
+        turn(9)
+        logits(4, 0)
+        logits(5, 0)
+        logits(6, 0)
+        logits(7, 0)
+        turn(10)
+        turn(11)
+        logits(0, 1)
+        logits(1, 1)
+        logits(2, 1)
+        logits(3, 1)
+        untangle(8)
+        untangle(9)
+        deviate(4, 0)
+        deviate(5, 0)
+        deviate(6, 0)
+        deviate(7, 0)
+        untangle(10)
+        untangle(11)
+        deviate(0, 1)
+        deviate(1, 1)
+        deviate(2, 1)
+        deviate(3, 1)
+        quant_x(4)
+        widen(12)
+        widen(13)
+        weight(0, 0)
+        quant_x(5)
+        widen(14)
+        widen(15)
+        quant_d(0, 0)
+        turn(12)
+        turn(13)
+        logits(8, 0)
+        logits(9, 0)
+        logits(4, 1)
+        logits(5, 1)
+        turn(14)
+        turn(15)
+        logits(10, 0)
+        logits(11, 0)
+        logits(6, 1)
+        logits(7, 1)
+        untangle(12)
+        untangle(13)
+        deviate(8, 0)
+        deviate(9, 0)
+        deviate(4, 1)
+        deviate(5, 1)
+        untangle(14)
+        untangle(15)
+        deviate(10, 0)
+        deviate(11, 0)
+        deviate(6, 1)
+        deviate(7, 1)
+        quant_x(6)
         quant_x(7)
-        pair_logits(7, 0)
-        weight(0, 1)
-        quant_d(2, 0)
-        pair_logits(5, 1)
-        open_half(2)
+        weight(1, 0)
+        weight(2, 0)
+        quant_d(1, 0)
+        logits(12, 0)
+        logits(13, 0)
+        logits(14, 0)
+        logits(15, 0)
+        gradient(0, 0, 0)
+        gradient(1, 0, 0)
+        gradient(2, 0, 0)
+        gradient(3, 0, 0)
+        logits(8, 1)
+        logits(9, 1)
+        logits(10, 1)
+        logits(11, 1)
+        gradient(0, 0, 1)
+        gradient(1, 0, 1)
+        gradient(2, 0, 1)
+        gradient(3, 0, 1)
+        logits(12, 1)
+        logits(13, 1)
+        logits(14, 1)
+        logits(15, 1)
+        deviate(12, 0)
+        deviate(13, 0)
+        deviate(14, 0)
+        deviate(15, 0)
+        deviate(8, 1)
+        deviate(9, 1)
+        deviate(10, 1)
+        deviate(11, 1)
+        deviate(12, 1)
+        deviate(13, 1)
+        deviate(14, 1)
+        deviate(15, 1)
         weight(3, 0)
-        quant_d(0, 1)
-        weight(1, 1)
+        quant_d(2, 0)
+        weight(0, 1)
         quant_d(3, 0)
-        pair_logits(6, 1)
-        pair_logits(7, 1)
-        for k in range(4):
-            gradient(k, 0, 3)
-            finish(k, 0, "s")
+        weight(1, 1)
+        quant_d(0, 1)
         weight(2, 1)
         quant_d(1, 1)
-        for k in range(4, 8):
-            for g in range(GROUPS):
-                gradient(k, 0, g)
-            finish(k, 0, "s")
-        all_half(0)
         weight(3, 1)
         quant_d(2, 1)
-        all_half(1)
         quant_d(3, 1)
-        all_half(2)
-        for k in range(8):
-            gradient(k, 1, 3)
-            finish(k, 1, "v" if k % 2 == 0 else "s")
+        gradient(0, 0, 2)
+        gradient(1, 0, 2)
+        gradient(2, 0, 2)
+        gradient(3, 0, 2)
+        gradient(4, 0, 0)
+        gradient(5, 0, 0)
+        gradient(6, 0, 0)
+        gradient(7, 0, 0)
+        gradient(4, 0, 1)
+        gradient(5, 0, 1)
+        gradient(6, 0, 1)
+        gradient(7, 0, 1)
+        gradient(0, 0, 3)
+        gradient(1, 0, 3)
+        gradient(2, 0, 3)
+        gradient(3, 0, 3)
+        gradient(4, 0, 2)
+        gradient(5, 0, 2)
+        gradient(6, 0, 2)
+        gradient(7, 0, 2)
+        gradient(4, 0, 3)
+        gradient(5, 0, 3)
+        gradient(6, 0, 3)
+        gradient(7, 0, 3)
+        gradient(0, 1, 0)
+        gradient(1, 1, 0)
+        gradient(2, 1, 0)
+        gradient(3, 1, 0)
+        gradient(4, 1, 0)
+        gradient(5, 1, 0)
+        gradient(6, 1, 0)
+        gradient(7, 1, 0)
+        gradient(0, 1, 1)
+        gradient(1, 1, 1)
+        gradient(2, 1, 1)
+        gradient(3, 1, 1)
+        gradient(4, 1, 1)
+        gradient(5, 1, 1)
+        gradient(6, 1, 1)
+        gradient(7, 1, 1)
+        gradient(0, 1, 2)
+        gradient(0, 1, 3)
+        gradient(1, 1, 2)
+        gradient(1, 1, 3)
+        gradient(2, 1, 2)
+        gradient(2, 1, 3)
+        gradient(3, 1, 2)
+        gradient(3, 1, 3)
+        gradient(4, 1, 2)
+        gradient(4, 1, 3)
+        gradient(5, 1, 2)
+        gradient(5, 1, 3)
+        gradient(6, 1, 2)
+        gradient(6, 1, 3)
+        gradient(7, 1, 2)
+        gradient(7, 1, 3)
+        finish(0, 0, "s")
+        finish(1, 0, "s")
+        finish(2, 0, "s")
+        finish(3, 0, "s")
+        finish(4, 0, "s")
+        finish(5, 0, "s")
+        finish(6, 0, "s")
+        finish(7, 0, "s")
+        finish(0, 1, "s")
+        finish(2, 1, "s")
+        finish(4, 1, "s")
+        finish(6, 1, "s")
+        finish(1, 1, "v")
+        finish(3, 1, "v")
+        finish(5, 1, "v")
+        finish(7, 1, "v")

from contextlib import ExitStack

import concourse.mybir as mybir
from concourse.masks import make_identity

TOKENS, HIDDEN, ACTIONS = 2048, 1024, 1024
FLOPS = 2 * 2 * TOKENS * HIDDEN * ACTIONS

F32 = mybir.dt.float32
BF16 = mybir.dt.bfloat16
I32 = mybir.dt.int32
U32 = mybir.dt.uint32
U8 = mybir.dt.uint8
FP8 = mybir.dt.float8_e4m3fn
FP8X4 = mybir.dt.float8_e4m3fn_x4
FP4X4 = mybir.dt.float4_e2m1fn_x4
MULT = mybir.AluOpType.mult
IDENTITY = mybir.ActivationFunctionType.Identity

P = 128
GROUPS = TOKENS // 512
TILES = TOKENS // P
PASSES = HIDDEN // 512
HALF = 512
CHUNKS = [slice(0, 512), slice(512, 1024)]


def tile_entropy_bonus_gradient_s13_kernel(
    tc, x_bytes, x_scale, w, mean_logit, rel_prob, coef, h_words, h_scales, out
):
    nc = tc.nc
    with ExitStack() as ctx:
        keep = ctx.enter_context(tc.tile_pool(name="keep", bufs=1))
        work = ctx.enter_context(tc.tile_pool(name="work", bufs=3))
        psum = ctx.enter_context(tc.psum_pool(name="psum", bufs=8))
        ctx.enter_context(tc.manual_schedule())

        ident = keep.tile([P, P], F32, name="ident")
        scale_row = keep.tile([P, HIDDEN], F32, name="scale_row", align_bytes=64)
        xb = [keep.tile([P, 4, HIDDEN], U8, name="xb%d" % g, align_bytes=64) for g in range(GROUPS)]
        w_raw = {}
        for h in range(2):
            for c in range(PASSES):
                w_raw[h, c] = keep.tile([P, 4, HALF], BF16, name="wr%d%d" % (h, c), align_bytes=64)
        rel = [keep.tile([P, 4, ACTIONS], BF16, name="rel%d" % g, align_bytes=64) for g in range(GROUPS)]
        hw = keep.tile([P, GROUPS, 2 * HIDDEN], U8, name="hw", align_bytes=64)
        hs = keep.tile([P, GROUPS, HIDDEN], U8, name="hs", align_bytes=64)
        mean_b = keep.tile([P, GROUPS, 4], BF16, name="mean_b")
        coef_b = keep.tile([P, GROUPS, 4], BF16, name="coef_b")
        coef_f = keep.tile([P, GROUPS, 4], F32, name="coef_f")
        mc = keep.tile([P, GROUPS, 4], F32, name="mc")
        nmc = keep.tile([P, GROUPS, 4], F32, name="nmc")
        warm = keep.tile([P, 1], F32, name="warm")

        xc = keep.tile([P, TILES, PASSES, P], U32, name="xc", align_bytes=64)
        xs = keep.tile([P, TILES, PASSES, P], U8, name="xs", align_bytes=64)
        wc = keep.tile([P, PASSES, ACTIONS], U32, name="wc", align_bytes=64)
        ws = keep.tile([P, PASSES, ACTIONS], U8, name="ws", align_bytes=64)
        dc = keep.tile([P, GROUPS, ACTIONS], U32, name="dc", align_bytes=64)
        ds = keep.tile([P, GROUPS, ACTIONS], U8, name="ds", align_bytes=64)

        def load_x(g, t0, t1):
            nc.sync.dma_start(
                out=xb[g][:, t0:t1, :],
                in_=x_bytes[512 * g : 512 * (g + 1), :].rearrange("(p t) k -> p t k", t=4)[:, t0:t1, :],
            )

        def load_w(h, c):
            nc.sync.dma_start(
                out=w_raw[h, c][:],
                in_=w[512 * c : 512 * (c + 1), HALF * h : HALF * (h + 1)].rearrange("(p j) n -> p j n", j=4),
            )

        def load_rel(g, t0, t1):
            nc.sync.dma_start(
                out=rel[g][:, t0:t1, :],
                in_=rel_prob[512 * g : 512 * (g + 1), :].rearrange("(p t) n -> p t n", t=4)[:, t0:t1, :],
            )

        nc.scalar.dma_start(out=mean_b[:], in_=mean_logit.rearrange("(g p t) -> p g t", p=P, t=4))
        nc.scalar.dma_start(out=coef_b[:], in_=coef.rearrange("(g p t) -> p g t", p=P, t=4))
        make_identity(nc, ident[:])
        nc.gpsimd.memset(warm[:], 0.0)
        nc.scalar.activation(out=warm[:], in_=warm[:], func=IDENTITY)
        nc.gpsimd.memset(hs[:].rearrange("p g n -> p (g n)").bitcast(U32), 0)
        nc.gpsimd.tensor_copy(out=coef_f[:], in_=coef_b[:])
        nc.gpsimd.tensor_tensor(out=mc[:], in0=mean_b[:], in1=coef_b[:], op=MULT)
        nc.gpsimd.tensor_scalar(out=nmc[:], in0=mc[:], scalar1=-1.0, scalar2=None, op0=MULT)

        nc.sync.dma_start(out=scale_row[:], in_=x_scale.rearrange("o k -> (o k)").partition_broadcast(P))
        load_x(0, 0, 2)
        load_w(0, 0)
        load_w(0, 1)
        load_x(0, 2, 4)
        load_x(1, 0, 4)
        load_x(2, 0, 4)
        load_x(3, 0, 4)
        load_w(1, 0)
        load_w(1, 1)
        for q in range(4):
            nc.sync.dma_start(
                out=hs[32 * q : 32 * q + 4].rearrange("p g n -> p (g n)").bitcast(I32).rearrange("p (g n) -> p g n", g=GROUPS),
                in_=h_scales[:, 4 * q : 4 * q + 4, :].rearrange("g q n -> q g n").bitcast(I32),
            )
        load_rel(0, 0, 2)
        load_rel(0, 2, 4)
        load_rel(1, 0, 4)
        nc.sync.dma_start(out=hw[:], in_=h_words.rearrange("g p c -> p g c"))
        load_rel(2, 0, 4)
        load_rel(3, 0, 4)

        xw = {}
        xt = {}
        xg = {}
        lg = {}
        dg = {}

        def widen(i):
            xw[i] = work.tile([P, HIDDEN], BF16, name="xw", tag="xw", bufs=4, align_bytes=64)
            nc.vector.tensor_tensor(
                out=xw[i][:], in0=xb[i // 4][:, i % 4, :].bitcast(FP8), in1=scale_row[:], op=MULT
            )

        def turn(i):
            xt[i] = psum.tile([P, 4, P], F32, name="bank", tag="bank", bufs=8)
            words = xw[i][:].bitcast(F32)
            for c in range(PASSES):
                for u in range(2):
                    nc.tensor.transpose(
                        xt[i][:, 2 * c + u, :], words[:, 256 * c + u : 256 * (c + 1) : 2], ident[:]
                    )

        def untangle(i):
            if i % 2 == 0:
                xg[i // 2] = work.tile([P, 2, PASSES * P * 4], BF16, name="xg", tag="xg", bufs=3, align_bytes=64)
            nc.scalar.copy(
                out=xg[i // 2][:, i % 2, :].bitcast(F32).rearrange("p (c r u) -> p c r u", c=PASSES, u=2),
                in_=xt[i][:].rearrange("p (c u) r -> p c r u", c=PASSES),
            )

        def quant_x(j):
            nc.vector.quantize_mx(
                out=xc[:, 2 * j : 2 * j + 2].rearrange("p a c r -> p (a c r)").bitcast(FP8X4),
                scales=xs[:, 2 * j : 2 * j + 2].rearrange("p a c r -> p (a c r)"),
                in_=xg[j][:].rearrange("p a f -> p (a f)"),
            )

        wg = {}

        def group_w(h, c, engine):
            wg[h, c] = work.tile([P, HALF, 4], BF16, name="wg", tag="wg", bufs=2, align_bytes=64)
            dst = wg[h, c][:].rearrange("p (c i) j -> p c j i", i=4)
            src = w_raw[h, c][:].rearrange("p j (c i) -> p c j i", i=4)
            if engine == "v":
                nc.vector.tensor_copy(out=dst, in_=src)
            else:
                nc.scalar.copy(out=dst, in_=src)

        def quant_w(h, c):
            cols = slice(HALF * h, HALF * (h + 1))
            nc.vector.quantize_mx(
                out=wc[:, c, cols].bitcast(FP8X4),
                scales=ws[:, c, cols],
                in_=wg[h, c][:].rearrange("p n j -> p (n j)"),
            )

        acc = {}

        def logits(i, h):
            acc[i, h] = psum.tile([P, HALF], F32, name="bank", tag="bank", bufs=8)
            cols = slice(HALF * h, HALF * (h + 1))
            for c in range(PASSES):
                nc.tensor.matmul_mx(
                    out=acc[i, h][:],
                    lhsT=xc[:, i, c, :].bitcast(FP8X4),
                    lhsT_scale=xs[:, i, c, :],
                    rhs=wc[:, c, cols].bitcast(FP8X4),
                    rhs_scale=ws[:, c, cols],
                    start=(c == 0),
                    stop=(c == PASSES - 1),
                )

        def deviate(i, h):
            g, t = i // 4, i % 4
            if t == 0:
                lg[g, h] = work.tile([P, 4, HALF], F32, name="lg", tag="lg", bufs=6, align_bytes=64)
            nc.scalar.activation(
                out=lg[g, h][:, t, :],
                in_=acc[i, h][:],
                func=IDENTITY,
                bias=nmc[:, g, t : t + 1],
                scale=coef_f[:, g, t : t + 1],
            )

        def weight(g, q):
            cols = CHUNKS[q]
            width = cols.stop - cols.start
            h = cols.start // HALF
            dg[g, q] = work.tile([P, width, 4], BF16, name="dg", tag="dg", bufs=3, align_bytes=64)
            nc.vector.tensor_tensor(
                out=dg[g, q][:].rearrange("p (c i) t -> p c t i", i=4),
                in0=lg[g, h][:, :, cols.start - HALF * h : cols.stop - HALF * h].rearrange("p t (c i) -> p c t i", i=4),
                in1=rel[g][:, :, cols].rearrange("p t (c i) -> p c t i", i=4),
                op=MULT,
            )

        def quant_d(g, q):
            cols = CHUNKS[q]
            nc.vector.quantize_mx(
                out=dc[:, g, cols].bitcast(FP8X4),
                scales=ds[:, g, cols],
                in_=dg[g, q][:].rearrange("p n t -> p (n t)"),
            )

        grad = {}

        def gradient(k, q, g):
            cols = CHUNKS[q]
            if g == 0:
                grad[k, q] = psum.tile([P, cols.stop - cols.start], F32, name="bank", tag="bank", bufs=8)
            nc.tensor.matmul_mx(
                out=grad[k, q][:],
                lhsT=hw[:, g, 2 * P * k : 2 * P * (k + 1)].bitcast(FP4X4),
                lhsT_scale=hs[:, g, P * k : P * (k + 1)],
                rhs=dc[:, g, cols].bitcast(FP8X4),
                rhs_scale=ds[:, g, cols],
                start=(g == 0),
                stop=(g == GROUPS - 1),
            )

        def finish(k, q, engine):
            cols = CHUNKS[q]
            res = work.tile([P, cols.stop - cols.start], F32, name="res", tag="res", bufs=8, align_bytes=64)
            if engine == "v":
                nc.vector.tensor_copy(out=res[:], in_=grad[k, q][:])
            else:
                nc.scalar.copy(out=res[:], in_=grad[k, q][:])
            nc.sync.dma_start(out=out[P * k : P * (k + 1), cols], in_=res[:])

        def pair_logits(j, h):
            logits(2 * j, h)
            logits(2 * j + 1, h)
            deviate(2 * j, h)
            deviate(2 * j + 1, h)

        widen(0)
        widen(1)
        widen(2)
        widen(3)
        turn(0)
        turn(1)
        turn(2)
        turn(3)
        group_w(0, 0, "s")
        untangle(0)
        untangle(1)
        group_w(0, 1, "s")
        untangle(2)
        untangle(3)
        group_w(1, 0, "s")
        quant_w(0, 0)
        widen(4)
        widen(5)
        quant_w(0, 1)
        quant_x(0)
        widen(6)
        widen(7)
        quant_x(1)
        turn(4)
        turn(5)
        turn(6)
        turn(7)
        logits(0, 0)
        logits(1, 0)
        logits(2, 0)
        logits(3, 0)
        untangle(4)
        untangle(5)
        untangle(6)
        untangle(7)
        group_w(1, 1, "s")
        deviate(0, 0)
        deviate(1, 0)
        deviate(2, 0)
        deviate(3, 0)
        quant_x(2)
        widen(8)
        widen(9)
        quant_w(1, 0)
        quant_x(3)
        widen(10)
        widen(11)
        quant_w(1, 1)
        turn(8)
        turn(9)
        logits(4, 0)
        logits(5, 0)
        logits(6, 0)
        logits(7, 0)
        turn(10)
        turn(11)
        logits(0, 1)
        logits(1, 1)
        logits(2, 1)
        logits(3, 1)
        untangle(8)
        untangle(9)
        deviate(4, 0)
        deviate(5, 0)
        deviate(6, 0)
        deviate(7, 0)
        untangle(10)
        untangle(11)
        deviate(0, 1)
        deviate(1, 1)
        deviate(2, 1)
        deviate(3, 1)
        quant_x(4)
        widen(12)
        widen(13)
        weight(0, 0)
        quant_x(5)
        widen(14)
        widen(15)
        quant_d(0, 0)
        turn(12)
        turn(13)
        logits(8, 0)
        logits(9, 0)
        logits(4, 1)
        logits(5, 1)
        turn(14)
        turn(15)
        logits(10, 0)
        logits(11, 0)
        logits(6, 1)
        logits(7, 1)
        untangle(12)
        untangle(13)
        deviate(8, 0)
        deviate(9, 0)
        deviate(4, 1)
        deviate(5, 1)
        untangle(14)
        untangle(15)
        deviate(10, 0)
        deviate(11, 0)
        deviate(6, 1)
        deviate(7, 1)
        quant_x(6)
        quant_x(7)
        weight(1, 0)
        weight(2, 0)
        quant_d(1, 0)
        logits(12, 0)
        logits(13, 0)
        logits(14, 0)
        logits(15, 0)
        gradient(0, 0, 0)
        gradient(1, 0, 0)
        gradient(2, 0, 0)
        gradient(3, 0, 0)
        logits(8, 1)
        logits(9, 1)
        logits(10, 1)
        logits(11, 1)
        gradient(0, 0, 1)
        gradient(1, 0, 1)
        gradient(2, 0, 1)
        gradient(3, 0, 1)
        logits(12, 1)
        logits(13, 1)
        logits(14, 1)
        logits(15, 1)
        deviate(12, 0)
        deviate(13, 0)
        deviate(14, 0)
        deviate(15, 0)
        deviate(8, 1)
        deviate(9, 1)
        deviate(10, 1)
        deviate(11, 1)
        deviate(12, 1)
        deviate(13, 1)
        deviate(14, 1)
        deviate(15, 1)
        weight(3, 0)
        quant_d(2, 0)
        weight(0, 1)
        quant_d(3, 0)
        weight(1, 1)
        quant_d(0, 1)
        weight(2, 1)
        quant_d(1, 1)
        weight(3, 1)
        quant_d(2, 1)
        quant_d(3, 1)
        gradient(0, 0, 2)
        gradient(1, 0, 2)
        gradient(2, 0, 2)
        gradient(3, 0, 2)
        gradient(4, 0, 0)
        gradient(5, 0, 0)
        gradient(6, 0, 0)
        gradient(7, 0, 0)
        gradient(4, 0, 1)
        gradient(5, 0, 1)
        gradient(6, 0, 1)
        gradient(7, 0, 1)
        gradient(0, 0, 3)
        gradient(1, 0, 3)
        gradient(2, 0, 3)
        gradient(3, 0, 3)
        gradient(4, 0, 2)
        gradient(5, 0, 2)
        gradient(6, 0, 2)
        gradient(7, 0, 2)
        gradient(4, 0, 3)
        gradient(5, 0, 3)
        gradient(6, 0, 3)
        gradient(7, 0, 3)
        gradient(0, 1, 0)
        gradient(1, 1, 0)
        gradient(2, 1, 0)
        gradient(3, 1, 0)
        gradient(4, 1, 0)
        gradient(5, 1, 0)
        gradient(6, 1, 0)
        gradient(7, 1, 0)
        gradient(0, 1, 1)
        gradient(1, 1, 1)
        gradient(2, 1, 1)
        gradient(3, 1, 1)
        gradient(4, 1, 1)
        gradient(5, 1, 1)
        gradient(6, 1, 1)
        gradient(7, 1, 1)
        gradient(0, 1, 2)
        gradient(0, 1, 3)
        gradient(1, 1, 2)
        gradient(1, 1, 3)
        gradient(2, 1, 2)
        gradient(2, 1, 3)
        gradient(3, 1, 2)
        gradient(3, 1, 3)
        gradient(4, 1, 2)
        gradient(4, 1, 3)
        gradient(5, 1, 2)
        gradient(5, 1, 3)
        gradient(6, 1, 2)
        gradient(6, 1, 3)
        gradient(7, 1, 2)
        gradient(7, 1, 3)
        finish(0, 0, "s")
        finish(1, 0, "s")
        finish(2, 0, "s")
        finish(3, 0, "s")
        finish(4, 0, "s")
        finish(5, 0, "s")
        finish(6, 0, "s")
        finish(7, 0, "s")
        finish(0, 1, "s")
        finish(2, 1, "s")
        finish(4, 1, "s")
        finish(6, 1, "s")
        finish(1, 1, "v")
        finish(3, 1, "v")
        finish(5, 1, "v")
        finish(7, 1, "v")
